import numpy as np
import ml_dtypes


def mxq(x, axis, fmt="e4m3"):
    dtype, down = {"e4m3": (ml_dtypes.float8_e4m3fn, 7), "e5m2": (ml_dtypes.float8_e5m2, 14)}[fmt]
    v = np.moveaxis(np.asarray(x, np.float32).astype(ml_dtypes.bfloat16).astype(np.float64), axis, -1)
    blocks = v.reshape(v.shape[:-1] + (-1, 32))
    amax = np.abs(blocks).max(-1, keepdims=True)
    byte = np.maximum(np.where(amax > 0, np.frexp(amax)[1] - 1 + 127, 0) - down, 1)
    scale = np.exp2(byte - 127.0)
    codes = (blocks / scale).astype(np.float32).astype(dtype).astype(np.float64)
    return np.moveaxis((codes * scale).reshape(v.shape), -1, axis)


WIDE = False


def mx_kscale(k):
    if not WIDE:
        return np.ones(k)
    levels = np.array([10, -10, 5, -5, 0])
    if k % 512:
        return np.exp2(np.random.permutation(np.resize(levels, k // 32))).repeat(32)
    a = np.empty((k // 512, 16))
    for p in range(k // 512):
        a[p, :8] = np.random.permutation(np.resize(levels, 8))
        for g in range(8):
            far = levels[np.abs(levels - a[p, g]) >= 10]
            a[p, g + 8] = far[np.random.randint(len(far))]
    return np.exp2(a.ravel()).repeat(32)


def f64(x):
    return np.asarray(x).astype(np.float64)


def striped(idx):
    return np.tile(np.asarray(idx).reshape(-1, 16).T, (8, 1)).astype(np.uint16)


def unstriped(offs):
    return offs[:16].T.reshape(-1).astype(np.int64)


def striped8(idx):
    return np.asarray(idx).reshape(8, -1, 16).transpose(0, 2, 1).reshape(128, -1).astype(np.uint16)


def unstriped8(offs):
    return offs.reshape(8, 16, -1).transpose(0, 2, 1).reshape(8, -1).astype(np.int64)


def pick8(x, idx, run):
    r = np.arange(len(x))
    return x[r[:, None], idx[r % (8 * run) // run]]


E2M1 = np.array([0.0, 0.5, 1.0, 1.5, 2.0, 3.0, 4.0, 6.0, -0.0, -0.5, -1.0, -1.5, -2.0, -3.0, -4.0, -6.0])


def pack_weight(w, fmt):
    k, n = w.shape
    w = f64(np.asarray(w, np.float32).astype(ml_dtypes.bfloat16)).reshape(k // 32, 32, n)
    amax = np.abs(w).max(1)
    if fmt == "e4m3":
        byte = np.frexp(amax)[1] - 1 + 127 - 7
    else:
        mant, ex = np.frexp(amax / 6.0)
        byte = np.where(mant > 0.5, ex, ex - 1) + 127
    byte = np.clip(np.where(amax > 0, byte, 1), 1, 254)
    scaled = (w * np.exp2(127.0 - byte)[:, None, :]).reshape(k, n).astype(np.float32)
    by_word = np.ascontiguousarray(scaled.reshape(k // 512, 128, 4, n).transpose(0, 1, 3, 2))
    if fmt == "e4m3":
        words = by_word.astype(ml_dtypes.float8_e4m3fn).view(np.uint8)
    else:
        c = by_word.astype(ml_dtypes.float4_e2m1fn).view(np.uint8) & 0xF
        words = (c[..., 0::2] | (c[..., 1::2] << 4)).reshape(k // 512, 128, 2 * n)
    return np.ascontiguousarray(words), np.ascontiguousarray(byte.astype(np.uint8).reshape(k // 512, 16, n))


def unpack_weight(words, scales, fmt):
    g, _, n = scales.shape
    words = np.ascontiguousarray(words).reshape(g, 128, n, -1)
    if fmt == "e4m3":
        vals = words.view(ml_dtypes.float8_e4m3fn).astype(np.float64)
    else:
        nib = np.empty((g, 128, n, 4), np.uint8)
        nib[..., 0::2] = words & 0xF
        nib[..., 1::2] = words >> 4
        vals = E2M1[nib]
    vals = vals * np.repeat(np.exp2(scales.astype(np.float64) - 127.0), 8, axis=1)[..., None]
    return vals.transpose(0, 1, 3, 2).reshape(g * 512, n)


def sigmoid(v):
    return 1.0 / (1.0 + np.exp(-v))


def bf(x):
    return np.asarray(x, np.float32).astype(ml_dtypes.bfloat16)


def planes(Y):
    r, m = Y.shape
    b = f64(bf(Y)).reshape(r // 32, 32, m)
    amax = np.abs(b).max(1)
    byte = np.clip(np.where(amax > 0, np.frexp(amax)[1] - 1 + 127 - 7, 1), 1, 254)
    codes = (b * np.exp2(127.0 - byte)[:, None, :]).reshape(r, m).astype(np.float32).astype(ml_dtypes.float8_e4m3fn).view(np.uint8)
    words = codes.reshape(r // 512, 128, 4, m).transpose(0, 1, 3, 2)
    return np.ascontiguousarray(words), np.ascontiguousarray(byte.astype(np.uint8).reshape(r // 512, 16, m))


K, R, F, T, J, M = 512, 512, 512, 2048, 512, 128


def setup_inputs():
    n = np.random.standard_normal
    idx = np.random.permutation(T)[:J]
    idx2 = np.stack([np.random.permutation(J)[:M] for _ in range(8)])
    idx3 = np.stack([np.random.permutation(J)[:M] for _ in range(8)])
    fk = mx_kscale(K)
    fr = mx_kscale(R)
    dtabp = pack_weight(n((K, T)) / fk[:, None], "e4m3")
    tabp = pack_weight(n((K, T)) / fk[:, None], "e4m3")
    return {
        "dtab_words": dtabp[0],
        "dtab_scales": dtabp[1],
        "tab_words": tabp[0],
        "tab_scales": tabp[1],
        "w1": (n((K, R)) * 1 / np.sqrt(K) * fk[:, None]).astype(np.float32),
        "gain": (np.random.uniform(0.5, 1.5, (R, 1))).astype(np.float32),
        "rs": (np.random.uniform(0.5, 2.0, (R, 1)) * fr[:, None]).astype(np.float32),
        "wor": (n((R, F)) * 1 / np.sqrt(R) / fr[:, None]).astype(np.float32),
        "res": (n((F, M)) * 0.5).astype(np.float32),
        "offs": striped(idx),
        "offs2": striped8(idx2),
        "offs3": striped8(idx3),
    }


def reference(dtab_words, dtab_scales, tab_words, tab_scales, w1, gain, rs, wor, res, offs, offs2, offs3):
    idx = unstriped(offs)
    idx2 = unstriped8(offs2)
    idx3 = unstriped8(offs3)
    dtabu = unpack_weight(dtab_words, dtab_scales, "e4m3")
    tabu = unpack_weight(tab_words, tab_scales, "e4m3")
    w1q = mxq(f64(w1), 0, "e4m3")
    tabidxg = tabu[:, idx]
    a = w1q.T @ tabidxg
    dtabidxg = dtabu[:, idx]
    ta = w1q.T @ dtabidxg
    h1 = a * f64(gain)
    th1 = ta * f64(gain)
    tu1 = pick8(th1, idx2, 64) * sigmoid(pick8(h1, idx3, 64)) + pick8(th1, idx3, 64) * sigmoid(pick8(h1, idx3, 64)) * (1.0 - sigmoid(pick8(h1, idx3, 64))) * pick8(h1, idx2, 64) - pick8(th1, idx3, 64) * sigmoid(pick8(h1, idx3, 64))
    fo1 = tu1 * f64(rs)
    worq = mxq(f64(wor), 0, "e4m3")
    fo1q = mxq(fo1, 0, "e4m3")
    yo = worq.T @ fo1q
    y = yo + f64(res)
    words, scales = planes(y)
    return y, words, scales

@@ -1,0 +1,167 @@
+from contextlib import ExitStack
+
+import concourse.mybir as mybir
+
+K, R, F, T, J, M = 512, 512, 512, 2048, 512, 128
+FLOPS = 2 * (2 * K * R * J + R * F * M)
+
+F32 = mybir.dt.float32
+BF16 = mybir.dt.bfloat16
+I32 = mybir.dt.int32
+U32 = mybir.dt.uint32
+U16 = mybir.dt.uint16
+U8 = mybir.dt.uint8
+FP8X4 = mybir.dt.float8_e4m3fn_x4
+ALU = mybir.AluOpType
+ACT = mybir.ActivationFunctionType
+
+P = 128
+PACK = 4
+W1_SPLIT = 48
+WOR_SPLIT = 64
+DTAB_ROW = 4
+
+
+def deal(engine_copy, dealt, raw, lo, hi):
+    engine_copy(
+        out=dealt[:].rearrange("p t m j -> p m j t")[:, lo:hi],
+        in_=raw[:].rearrange("p j (m t) -> p m j t", t=PACK)[:, lo:hi],
+    )
+
+
+def tile_attend_tpairgates_o_pl_kernel(tc, dtab_words, dtab_scales, tab_words, tab_scales, w1, gain, rs, wor, res,
+                                        offs, offs2, offs3, out_0, out_1, out_2):
+    nc = tc.nc
+    with ExitStack() as ctx:
+        pool = ctx.enter_context(tc.tile_pool(name="keep", bufs=1))
+        psum = ctx.enter_context(tc.psum_pool(name="psum", bufs=1))
+
+        slot_list = pool.tile([P, J // 16], U16)
+        pick2 = pool.tile([P, M // 16], U16)
+        pick3 = pool.tile([P, M // 16], U16)
+        tab_w = pool.tile([P, T], U32, align_bytes=64, tag="tab_w")
+        dtab_w = pool.tile([P, T], U32, align_bytes=64, tag="dtab_w")
+        tab_s = pool.tile([P, T], U8, align_bytes=64)
+        dtab_s = pool.tile([P, T], U8, align_bytes=64, tag="dtab_s")
+        w1_raw = pool.tile([P, PACK, R], F32, align_bytes=64)
+        gain_sb = pool.tile([P, PACK], F32)
+        rs_sb = pool.tile([P, PACK], F32)
+
+        nc.gpsimd.memset(tab_s[:].bitcast(I32), 0)
+        nc.vector.memset(dtab_s[:].bitcast(I32), 0)
+
+        nc.sync.dma_start(slot_list[:], offs)
+        nc.scalar.dma_start(out=w1_raw[:], in_=w1.rearrange("(p j) c -> p j c", j=PACK))
+        nc.scalar.dma_start(out=tab_w[:].bitcast(I32), in_=tab_words[0].rearrange("p n t -> p (n t)").bitcast(I32))
+        nc.scalar.dma_start(out=dtab_w[:].bitcast(I32), in_=dtab_words[0].rearrange("p n t -> p (n t)").bitcast(I32))
+        for q in range(4):
+            queue = nc.gpsimd if q == 3 else nc.sync
+            queue.dma_start(out=tab_s[32 * q : 32 * q + 4, :].bitcast(I32),
+                            in_=tab_scales[0, 4 * q : 4 * q + 4, :].bitcast(I32))
+        for q in range(4):
+            queue = nc.gpsimd if q == 3 else nc.sync
+            queue.dma_start(out=dtab_s[32 * q + DTAB_ROW : 32 * q + DTAB_ROW + 4, :].bitcast(I32),
+                            in_=dtab_scales[0, 4 * q : 4 * q + 4, :].bitcast(I32))
+        nc.gpsimd.dma_start(out=gain_sb[:], in_=gain.rearrange("(p t) o -> p (t o)", t=PACK))
+        nc.gpsimd.dma_start(out=rs_sb[:], in_=rs.rearrange("(p t) o -> p (t o)", t=PACK))
+        nc.sync.dma_start(pick3[:], offs3)
+        nc.sync.dma_start(pick2[:], offs2)
+
+        warm = pool.tile([P, 1], F32)
+        warm_out = pool.tile([P, 1], F32)
+        nc.vector.memset(warm[:], 0.0)
+        nc.scalar.activation(out=warm_out[:], in_=warm[:], func=ACT.Sigmoid)
+
+        tab_gw = pool.tile([P, J], U32, align_bytes=64)
+        dtab_gw = pool.tile([P, J], U32, align_bytes=64)
+        tab_gs = pool.tile([P, J], U8, align_bytes=64)
+        nc.vector.tensor_copy(tab_gs[:], tab_s[:].indirect(slot_list[:]))
+
+        w1_bf = pool.tile([P, PACK, P, PACK], BF16, align_bytes=64)
+        w1_q = pool.tile([P, R], U32, align_bytes=64)
+        w1_s = pool.tile([P, R], U8, align_bytes=64)
+        deal(nc.scalar.copy, w1_bf, w1_raw, 0, W1_SPLIT)
+        deal(nc.vector.tensor_copy, w1_bf, w1_raw, W1_SPLIT, P)
+        nc.vector.quantize_mx(out=w1_q[:].bitcast(FP8X4), scales=w1_s[:],
+                              in_=w1_bf[:].rearrange("p t m j -> p (t m j)"))
+        nc.vector.tensor_copy(tab_gw[:], tab_w[:].indirect(slot_list[:]))
+        dtab_gs = pool.tile([P, J], U8, align_bytes=64, tag="tab_w")
+        nc.vector.tensor_copy(dtab_gs[:], dtab_s[:].indirect(slot_list[:]))
+        wor_raw = pool.tile([P, PACK, F], F32, align_bytes=64, tag="dtab_s")
+        nc.sync.dma_start(out=wor_raw[:], in_=wor.rearrange("(p j) c -> p j c", j=PACK))
+
+        def first_layer(t, words, scales, tag):
+            bank = psum.tile([P, J], F32, name=tag, tag=tag)
+            cols = slice(t * P, (t + 1) * P)
+            nc.tensor.matmul_mx(out=bank[:], lhsT=w1_q[:, cols].bitcast(FP8X4), lhsT_scale=w1_s[:, cols],
+                                rhs=words[:].bitcast(FP8X4), rhs_scale=scales, start=True, stop=True)
+            return bank
+
+        a_banks = [first_layer(t, tab_gw, tab_gs[:], "a%d" % t) for t in range(PACK)]
+        nc.vector.tensor_copy(dtab_gw[:], dtab_w[:].indirect(slot_list[:]))
+        res_sb = pool.tile([P, PACK, M], F32, align_bytes=64, tag="dtab_w")
+        nc.sync.dma_start(out=res_sb[:], in_=res.rearrange("(p t) m -> p t m", t=PACK))
+        ta_banks = [first_layer(t, dtab_gw, dtab_gs[DTAB_ROW:P, :], "ta%d" % t) for t in range(PACK)]
+
+        h1 = [pool.tile([P, J], F32, name="h1_%d" % t, align_bytes=64) for t in range(PACK)]
+        th1 = [pool.tile([P, J], F32, name="th1_%d" % t, align_bytes=64) for t in range(PACK)]
+        sig = pool.tile([P, PACK, M], F32, align_bytes=64)
+        rest = pool.tile([P, PACK, M], F32, align_bytes=64)
+        sig_rs = pool.tile([P, PACK, M], F32, align_bytes=64)
+        prod = pool.tile([P, PACK, M], F32, align_bytes=64)
+        slope = pool.tile([P, PACK, M], F32, align_bytes=64)
+        part = pool.tile([P, PACK, M], F32, align_bytes=64)
+        total = pool.tile([P, PACK, M], F32, align_bytes=64)
+
+        for t in range(PACK):
+            nc.scalar.activation(out=h1[t][:], in_=a_banks[t][:], func=ACT.Copy, scale=gain_sb[:, t : t + 1])
+            nc.scalar.activation(out=sig[:, t, :], in_=h1[t][:].indirect(pick3[:]), func=ACT.Sigmoid)
+            nc.scalar.activation(out=rest[:, t, :], in_=sig[:, t, :], func=ACT.Copy, scale=-1.0, bias=1.0)
+        nc.vector.tensor_scalar(th1[0][:], ta_banks[0][:], gain_sb[:, 0:1], None, ALU.mult)
+        for t in range(PACK):
+            nc.vector.tensor_tensor(prod[:, t, :], h1[t][:].indirect(pick2[:]), rest[:, t, :], ALU.mult)
+        for t in range(1, PACK):
+            nc.scalar.activation(out=th1[t][:], in_=ta_banks[t][:], func=ACT.Copy, scale=gain_sb[:, t : t + 1])
+        nc.vector.tensor_scalar(slope[:], prod[:], -1.0, None, ALU.add)
+        for t in range(PACK):
+            nc.scalar.activation(out=sig_rs[:, t, :], in_=sig[:, t, :], func=ACT.Copy, scale=rs_sb[:, t : t + 1])
+
+        wor_bf = pool.tile([P, PACK, P, PACK], BF16, align_bytes=64)
+        wor_q = pool.tile([P, F], U32, align_bytes=64)
+        wor_s = pool.tile([P, F], U8, align_bytes=64)
+        deal(nc.vector.tensor_copy, wor_bf, wor_raw, 0, WOR_SPLIT)
+        deal(nc.scalar.copy, wor_bf, wor_raw, WOR_SPLIT, P)
+
+        for t in range(PACK):
+            nc.vector.tensor_tensor(part[:, t, :], th1[t][:].indirect(pick3[:]), slope[:, t, :], ALU.mult)
+            if t > 0:
+                nc.vector.tensor_tensor(total[:, t - 1, :], th1[t - 1][:].indirect(pick2[:]), part[:, t - 1, :], ALU.add)
+        nc.vector.quantize_mx(out=wor_q[:].bitcast(FP8X4), scales=wor_s[:],
+                              in_=wor_bf[:].rearrange("p t m j -> p (t m j)"))
+        nc.vector.tensor_tensor(total[:, PACK - 1, :], th1[PACK - 1][:].indirect(pick2[:]), part[:, PACK - 1, :], ALU.add)
+
+        fo_bf = pool.tile([P, M, PACK], BF16, align_bytes=64)
+        fo_q = pool.tile([P, M], U32, align_bytes=64)
+        fo_s = pool.tile([P, M], U8, align_bytes=64)
+        nc.vector.tensor_tensor(fo_bf[:].rearrange("p (c i) t -> p c t i", i=4),
+                                total[:].rearrange("p t (c i) -> p c t i", i=4),
+                                sig_rs[:].rearrange("p t (c i) -> p c t i", i=4), ALU.mult)
+        nc.vector.quantize_mx(out=fo_q[:].bitcast(FP8X4), scales=fo_s[:], in_=fo_bf[:].rearrange("p m t -> p (m t)"))
+
+        yo = psum.tile([P, PACK, M], F32, name="a0", tag="a0")
+        for t in range(PACK):
+            cols = slice(t * P, (t + 1) * P)
+            nc.tensor.matmul_mx(out=yo[:, t, :], lhsT=wor_q[:, cols].bitcast(FP8X4), lhsT_scale=wor_s[:, cols],
+                                rhs=fo_q[:].bitcast(FP8X4), rhs_scale=fo_s[:], start=True, stop=True)
+        y = pool.tile([P, PACK, M], F32, align_bytes=64)
+        nc.vector.tensor_tensor(y[:], yo[:], res_sb[:], ALU.add)
+        nc.sync.dma_start(out=out_0.rearrange("(p t) m -> p t m", t=PACK), in_=y[:])
+        y_bf = pool.tile([P, M, PACK], BF16, align_bytes=64)
+        y_q = pool.tile([P, M], U32, align_bytes=64)
+        y_s = pool.tile([P, M], U8, align_bytes=64)
+        nc.vector.tensor_copy(y_bf[:].rearrange("p (c i) t -> p c t i", i=4), y[:].rearrange("p t (c i) -> p c t i", i=4))
+        nc.vector.quantize_mx(out=y_q[:].bitcast(FP8X4), scales=y_s[:], in_=y_bf[:].rearrange("p m t -> p (m t)"))
+        nc.sync.dma_start(out=out_1[0].rearrange("p c t -> p (c t)").bitcast(I32), in_=y_q[:].bitcast(I32))
+        for q in range(4):
+            queue = nc.scalar if q % 2 == 0 else nc.sync
+            queue.dma_start(out=out_2[0, 4 * q : 4 * q + 4, :].bitcast(I32), in_=y_s[32 * q : 32 * q + 4, :].bitcast(I32))

@@ -17,15 +17,15 @@ ACT = mybir.ActivationFunctionType
 
 P = 128
 PACK = 4
-W1_SPLIT = 48
-WOR_SPLIT = 64
+W1_SPLIT = 96
 DTAB_ROW = 4
+HALF = J // 2
 
 
-def deal(engine_copy, dealt, raw, lo, hi):
+def deal(engine_copy, dealt, raw, lo, hi, first=0):
     engine_copy(
         out=dealt[:].rearrange("p t m j -> p m j t")[:, lo:hi],
-        in_=raw[:].rearrange("p j (m t) -> p m j t", t=PACK)[:, lo:hi],
+        in_=raw[:].rearrange("p j (m t) -> p m j t", t=PACK)[:, lo - first : hi - first],
     )
 
 
@@ -41,106 +41,117 @@ def tile_attend_tpairgates_o_pl_kernel(tc, dtab_words, dtab_scales, tab_words, t
         pick3 = pool.tile([P, M // 16], U16)
         tab_w = pool.tile([P, T], U32, align_bytes=64, tag="tab_w")
         dtab_w = pool.tile([P, T], U32, align_bytes=64, tag="dtab_w")
-        tab_s = pool.tile([P, T], U8, align_bytes=64)
-        dtab_s = pool.tile([P, T], U8, align_bytes=64, tag="dtab_s")
+        tab_s = pool.tile([P, T], U8, align_bytes=64, tag="tab_s")
+        dtab_s = pool.tile([P, T], U8, align_bytes=64)
         w1_raw = pool.tile([P, PACK, R], F32, align_bytes=64)
+        wor_lo = pool.tile([P, PACK, F // 2], F32, align_bytes=64, tag="h1_1")
+        wor_hi = pool.tile([P, PACK, F // 2], F32, align_bytes=64)
+        wor_rows = wor.rearrange("(p j) c -> p j c", j=PACK)
+        res_sb = pool.tile([P, PACK, M], F32, align_bytes=64)
         gain_sb = pool.tile([P, PACK], F32)
         rs_sb = pool.tile([P, PACK], F32)
 
-        nc.gpsimd.memset(tab_s[:].bitcast(I32), 0)
-        nc.vector.memset(dtab_s[:].bitcast(I32), 0)
-
-        nc.sync.dma_start(slot_list[:], offs)
-        nc.scalar.dma_start(out=w1_raw[:], in_=w1.rearrange("(p j) c -> p j c", j=PACK))
-        nc.scalar.dma_start(out=tab_w[:].bitcast(I32), in_=tab_words[0].rearrange("p n t -> p (n t)").bitcast(I32))
-        nc.scalar.dma_start(out=dtab_w[:].bitcast(I32), in_=dtab_words[0].rearrange("p n t -> p (n t)").bitcast(I32))
-        for q in range(4):
-            queue = nc.gpsimd if q == 3 else nc.sync
-            queue.dma_start(out=tab_s[32 * q : 32 * q + 4, :].bitcast(I32),
-                            in_=tab_scales[0, 4 * q : 4 * q + 4, :].bitcast(I32))
-        for q in range(4):
-            queue = nc.gpsimd if q == 3 else nc.sync
-            queue.dma_start(out=dtab_s[32 * q + DTAB_ROW : 32 * q + DTAB_ROW + 4, :].bitcast(I32),
-                            in_=dtab_scales[0, 4 * q : 4 * q + 4, :].bitcast(I32))
-        nc.gpsimd.dma_start(out=gain_sb[:], in_=gain.rearrange("(p t) o -> p (t o)", t=PACK))
-        nc.gpsimd.dma_start(out=rs_sb[:], in_=rs.rearrange("(p t) o -> p (t o)", t=PACK))
-        nc.sync.dma_start(pick3[:], offs3)
-        nc.sync.dma_start(pick2[:], offs2)
-
         warm = pool.tile([P, 1], F32)
         warm_out = pool.tile([P, 1], F32)
+        nc.vector.memset(tab_s[:].bitcast(I32), 0)
+        nc.vector.memset(dtab_s[:].bitcast(I32), 0)
         nc.vector.memset(warm[:], 0.0)
+
+        nc.sync.dma_start(out=w1_raw[:], in_=w1.rearrange("(p j) c -> p j c", j=PACK))
+        nc.sync.dma_start(slot_list[:], offs)
+        nc.sync.dma_start(pick3[:], offs3)
         nc.scalar.activation(out=warm_out[:], in_=warm[:], func=ACT.Sigmoid)
+        for q in range(4):
+            nc.sync.dma_start(out=tab_s[32 * q : 32 * q + 4, :].bitcast(I32),
+                              in_=tab_scales[0, 4 * q : 4 * q + 4, :].bitcast(I32))
+        nc.sync.dma_start(out=tab_w[:].bitcast(I32), in_=tab_words[0].rearrange("p n t -> p (n t)").bitcast(I32))
+        nc.sync.dma_start(out=wor_lo[:], in_=wor_rows[:, :, 0 : F // 2])
+        for q in range(4):
+            nc.sync.dma_start(out=dtab_s[32 * q + DTAB_ROW : 32 * q + DTAB_ROW + 4, :].bitcast(I32),
+                              in_=dtab_scales[0, 4 * q : 4 * q + 4, :].bitcast(I32))
+        nc.sync.dma_start(out=gain_sb[:], in_=gain.rearrange("(p t) o -> p (t o)", t=PACK))
+        nc.sync.dma_start(out=dtab_w[:].bitcast(I32), in_=dtab_words[0].rearrange("p n t -> p (n t)").bitcast(I32))
+        nc.sync.dma_start(pick2[:], offs2)
+        nc.sync.dma_start(out=wor_hi[:], in_=wor_rows[:, :, F // 2 : F])
+        nc.sync.dma_start(out=res_sb[:], in_=res.rearrange("(p t) m -> p t m", t=PACK))
+        nc.sync.dma_start(out=rs_sb[:], in_=rs.rearrange("(p t) o -> p (t o)", t=PACK))
 
         tab_gw = pool.tile([P, J], U32, align_bytes=64)
         dtab_gw = pool.tile([P, J], U32, align_bytes=64)
         tab_gs = pool.tile([P, J], U8, align_bytes=64)
-        nc.vector.tensor_copy(tab_gs[:], tab_s[:].indirect(slot_list[:]))
 
+        nc.vector.tensor_copy(tab_gs[:], tab_s[:].indirect(slot_list[:]))
         w1_bf = pool.tile([P, PACK, P, PACK], BF16, align_bytes=64)
-        w1_q = pool.tile([P, R], U32, align_bytes=64)
+        w1_q = pool.tile([P, R], U32, align_bytes=64, tag="tab_s")
         w1_s = pool.tile([P, R], U8, align_bytes=64)
         deal(nc.scalar.copy, w1_bf, w1_raw, 0, W1_SPLIT)
         deal(nc.vector.tensor_copy, w1_bf, w1_raw, W1_SPLIT, P)
         nc.vector.quantize_mx(out=w1_q[:].bitcast(FP8X4), scales=w1_s[:],
                               in_=w1_bf[:].rearrange("p t m j -> p (t m j)"))
-        nc.vector.tensor_copy(tab_gw[:], tab_w[:].indirect(slot_list[:]))
-        dtab_gs = pool.tile([P, J], U8, align_bytes=64, tag="tab_w")
-        nc.vector.tensor_copy(dtab_gs[:], dtab_s[:].indirect(slot_list[:]))
-        wor_raw = pool.tile([P, PACK, F], F32, align_bytes=64, tag="dtab_s")
-        nc.sync.dma_start(out=wor_raw[:], in_=wor.rearrange("(p j) c -> p j c", j=PACK))
 
-        def first_layer(t, words, scales, tag):
-            bank = psum.tile([P, J], F32, name=tag, tag=tag)
-            cols = slice(t * P, (t + 1) * P)
-            nc.tensor.matmul_mx(out=bank[:], lhsT=w1_q[:, cols].bitcast(FP8X4), lhsT_scale=w1_s[:, cols],
-                                rhs=words[:].bitcast(FP8X4), rhs_scale=scales, start=True, stop=True)
-            return bank
+        def first_layer(table, words, scales, row, tag):
+            banks = [psum.tile([P, J], F32, name="%s%d" % (tag, t), tag="%s%d" % (tag, t)) for t in range(PACK)]
+            for half in range(2):
+                slots = slice(half * HALF, (half + 1) * HALF)
+                nc.vector.tensor_copy(words[:, slots],
+                                      table[:].indirect(slot_list[:, half * HALF // 16 : (half + 1) * HALF // 16]))
+                for t in range(PACK):
+                    cols = slice(t * P, (t + 1) * P)
+                    nc.tensor.matmul_mx(out=banks[t][:, slots], lhsT=w1_q[:, cols].bitcast(FP8X4), lhsT_scale=w1_s[:, cols],
+                                        rhs=words[:, slots].bitcast(FP8X4), rhs_scale=scales[row:P, slots],
+                                        start=True, stop=True)
+            return banks
 
-        a_banks = [first_layer(t, tab_gw, tab_gs[:], "a%d" % t) for t in range(PACK)]
-        nc.vector.tensor_copy(dtab_gw[:], dtab_w[:].indirect(slot_list[:]))
-        res_sb = pool.tile([P, PACK, M], F32, align_bytes=64, tag="dtab_w")
-        nc.sync.dma_start(out=res_sb[:], in_=res.rearrange("(p t) m -> p t m", t=PACK))
-        ta_banks = [first_layer(t, dtab_gw, dtab_gs[DTAB_ROW:P, :], "ta%d" % t) for t in range(PACK)]
-
-        h1 = [pool.tile([P, J], F32, name="h1_%d" % t, align_bytes=64) for t in range(PACK)]
+        wor_bf = pool.tile([P, PACK, P, PACK], BF16, align_bytes=64, tag="wor_bf")
+        deal(nc.scalar.copy, wor_bf, wor_lo, 0, P // 2)
+        h1 = [pool.tile([P, J], F32, name="h1_%d" % t, tag="h1_%d" % t, align_bytes=64) for t in range(PACK)]
         th1 = [pool.tile([P, J], F32, name="th1_%d" % t, align_bytes=64) for t in range(PACK)]
         sig = pool.tile([P, PACK, M], F32, align_bytes=64)
         rest = pool.tile([P, PACK, M], F32, align_bytes=64)
         sig_rs = pool.tile([P, PACK, M], F32, align_bytes=64)
-        prod = pool.tile([P, PACK, M], F32, align_bytes=64)
         slope = pool.tile([P, PACK, M], F32, align_bytes=64)
         part = pool.tile([P, PACK, M], F32, align_bytes=64)
         total = pool.tile([P, PACK, M], F32, align_bytes=64)
-
-        for t in range(PACK):
-            nc.scalar.activation(out=h1[t][:], in_=a_banks[t][:], func=ACT.Copy, scale=gain_sb[:, t : t + 1])
-            nc.scalar.activation(out=sig[:, t, :], in_=h1[t][:].indirect(pick3[:]), func=ACT.Sigmoid)
-            nc.scalar.activation(out=rest[:, t, :], in_=sig[:, t, :], func=ACT.Copy, scale=-1.0, bias=1.0)
-        nc.vector.tensor_scalar(th1[0][:], ta_banks[0][:], gain_sb[:, 0:1], None, ALU.mult)
-        for t in range(PACK):
-            nc.vector.tensor_tensor(prod[:, t, :], h1[t][:].indirect(pick2[:]), rest[:, t, :], ALU.mult)
-        for t in range(1, PACK):
-            nc.scalar.activation(out=th1[t][:], in_=ta_banks[t][:], func=ACT.Copy, scale=gain_sb[:, t : t + 1])
-        nc.vector.tensor_scalar(slope[:], prod[:], -1.0, None, ALU.add)
-        for t in range(PACK):
-            nc.scalar.activation(out=sig_rs[:, t, :], in_=sig[:, t, :], func=ACT.Copy, scale=rs_sb[:, t : t + 1])
-
-        wor_bf = pool.tile([P, PACK, P, PACK], BF16, align_bytes=64)
         wor_q = pool.tile([P, F], U32, align_bytes=64)
         wor_s = pool.tile([P, F], U8, align_bytes=64)
-        deal(nc.vector.tensor_copy, wor_bf, wor_raw, 0, WOR_SPLIT)
-        deal(nc.scalar.copy, wor_bf, wor_raw, WOR_SPLIT, P)
+
+        a_banks = first_layer(tab_w, tab_gw, tab_gs, 0, "a")
+        dtab_gs = pool.tile([P, J], U8, align_bytes=64, tag="tab_w")
+        nc.vector.tensor_copy(dtab_gs[:], dtab_s[:].indirect(slot_list[:]))
+        nc.vector.tensor_scalar(h1[0][:], a_banks[0][:], gain_sb[:, 0:1], None, ALU.mult)
+        ta_banks = first_layer(dtab_w, dtab_gw, dtab_gs, DTAB_ROW, "ta")
+        prod = pool.tile([P, PACK, M], F32, align_bytes=64, tag="dtab_w")
+
+        def gained(dst, bank, t):
+            nc.scalar.activation(out=dst[:], in_=bank[:], func=ACT.Copy, scale=gain_sb[:, t : t + 1])
+
+        def gate(t):
+            nc.scalar.activation(out=sig[:, t, :], in_=h1[t][:].indirect(pick3[:]), func=ACT.Sigmoid)
+            nc.scalar.activation(out=rest[:, t, :], in_=sig[:, t, :], func=ACT.Copy, scale=-1.0, bias=1.0)
+            nc.vector.tensor_tensor(prod[:, t, :], h1[t][:].indirect(pick2[:]), rest[:, t, :], ALU.mult)
 
         for t in range(PACK):
+            if t + 1 < PACK:
+                gained(h1[t + 1], a_banks[t + 1], t + 1)
+            gate(t)
+            if t % 2 == 1:
+                nc.vector.tensor_scalar(slope[:, t - 1 : t + 1, :], prod[:, t - 1 : t + 1, :], -1.0, None, ALU.add)
+            if t == 1:
+                nc.vector.tensor_scalar(th1[0][:], ta_banks[0][:], gain_sb[:, 0:1], None, ALU.mult)
+        for t in range(PACK):
+            if t + 1 < PACK:
+                gained(th1[t + 1], ta_banks[t + 1], t + 1)
             nc.vector.tensor_tensor(part[:, t, :], th1[t][:].indirect(pick3[:]), slope[:, t, :], ALU.mult)
             if t > 0:
                 nc.vector.tensor_tensor(total[:, t - 1, :], th1[t - 1][:].indirect(pick2[:]), part[:, t - 1, :], ALU.add)
+        deal(nc.scalar.copy, wor_bf, wor_hi, P // 2, P, P // 2)
+        for t in range(PACK):
+            nc.scalar.activation(out=sig_rs[:, t, :], in_=sig[:, t, :], func=ACT.Copy, scale=rs_sb[:, t : t + 1])
         nc.vector.quantize_mx(out=wor_q[:].bitcast(FP8X4), scales=wor_s[:],
                               in_=wor_bf[:].rearrange("p t m j -> p (t m j)"))
         nc.vector.tensor_tensor(total[:, PACK - 1, :], th1[PACK - 1][:].indirect(pick2[:]), part[:, PACK - 1, :], ALU.add)
 
-        fo_bf = pool.tile([P, M, PACK], BF16, align_bytes=64)
+        fo_bf = pool.tile([P, M, PACK], BF16, align_bytes=64, tag="wor_bf")
         fo_q = pool.tile([P, M], U32, align_bytes=64)
         fo_s = pool.tile([P, M], U8, align_bytes=64)
         nc.vector.tensor_tensor(fo_bf[:].rearrange("p (c i) t -> p c t i", i=4),

@@ -77,7 +77,7 @@ def tile_attend_tpairgates_o_pl_kernel(tc, dtab_words, dtab_scales, tab_words, t
         nc.sync.dma_start(out=rs_sb[:], in_=rs.rearrange("(p t) o -> p (t o)", t=PACK))
 
         tab_gw = pool.tile([P, J], U32, align_bytes=64)
-        dtab_gw = pool.tile([P, J], U32, align_bytes=64)
+        dtab_gw = pool.tile([P, J], U32, align_bytes=64, tag="h1_3")
         tab_gs = pool.tile([P, J], U8, align_bytes=64)
 
         nc.vector.tensor_copy(tab_gs[:], tab_s[:].indirect(slot_list[:]))
@@ -102,9 +102,9 @@ def tile_attend_tpairgates_o_pl_kernel(tc, dtab_words, dtab_scales, tab_words, t
                                         start=True, stop=True)
             return banks
 
-        wor_bf = pool.tile([P, PACK, P, PACK], BF16, align_bytes=64, tag="wor_bf")
+        wor_bf = pool.tile([P, PACK, P, PACK], BF16, align_bytes=64)
         deal(nc.scalar.copy, wor_bf, wor_lo, 0, P // 2)
-        h1 = [pool.tile([P, J], F32, name="h1_%d" % t, tag="h1_%d" % t, align_bytes=64) for t in range(PACK)]
+        h1 = [pool.tile([P, J], F32, name="h1_%d" % t, tag="h1_%d" % t, align_bytes=64) for t in range(PACK - 1)]
         th1 = [pool.tile([P, J], F32, name="th1_%d" % t, align_bytes=64) for t in range(PACK)]
         sig = pool.tile([P, PACK, M], F32, align_bytes=64)
         rest = pool.tile([P, PACK, M], F32, align_bytes=64)
@@ -112,8 +112,6 @@ def tile_attend_tpairgates_o_pl_kernel(tc, dtab_words, dtab_scales, tab_words, t
         slope = pool.tile([P, PACK, M], F32, align_bytes=64)
         part = pool.tile([P, PACK, M], F32, align_bytes=64)
         total = pool.tile([P, PACK, M], F32, align_bytes=64)
-        wor_q = pool.tile([P, F], U32, align_bytes=64)
-        wor_s = pool.tile([P, F], U8, align_bytes=64)
 
         a_banks = first_layer(tab_w, tab_gw, tab_gs, 0, "a")
         dtab_gs = pool.tile([P, J], U8, align_bytes=64, tag="tab_w")
@@ -121,6 +119,7 @@ def tile_attend_tpairgates_o_pl_kernel(tc, dtab_words, dtab_scales, tab_words, t
         nc.vector.tensor_scalar(h1[0][:], a_banks[0][:], gain_sb[:, 0:1], None, ALU.mult)
         ta_banks = first_layer(dtab_w, dtab_gw, dtab_gs, DTAB_ROW, "ta")
         prod = pool.tile([P, PACK, M], F32, align_bytes=64, tag="dtab_w")
+        h1.append(pool.tile([P, J], F32, name="h1_3", tag="h1_3", align_bytes=64))
 
         def gained(dst, bank, t):
             nc.scalar.activation(out=dst[:], in_=bank[:], func=ACT.Copy, scale=gain_sb[:, t : t + 1])
@@ -130,42 +129,58 @@ def tile_attend_tpairgates_o_pl_kernel(tc, dtab_words, dtab_scales, tab_words, t
             nc.scalar.activation(out=rest[:, t, :], in_=sig[:, t, :], func=ACT.Copy, scale=-1.0, bias=1.0)
             nc.vector.tensor_tensor(prod[:, t, :], h1[t][:].indirect(pick2[:]), rest[:, t, :], ALU.mult)
 
-        for t in range(PACK):
-            if t + 1 < PACK:
-                gained(h1[t + 1], a_banks[t + 1], t + 1)
+        def less_one(pair):
+            rows = slice(2 * pair, 2 * pair + 2)
+            nc.vector.tensor_scalar(slope[:, rows, :], prod[:, rows, :], -1.0, None, ALU.add)
+
+        gained(h1[1], a_banks[1], 1)
+        gained(h1[2], a_banks[2], 2)
+        for t in range(PACK - 1):
             gate(t)
-            if t % 2 == 1:
-                nc.vector.tensor_scalar(slope[:, t - 1 : t + 1, :], prod[:, t - 1 : t + 1, :], -1.0, None, ALU.add)
-            if t == 1:
-                nc.vector.tensor_scalar(th1[0][:], ta_banks[0][:], gain_sb[:, 0:1], None, ALU.mult)
+        less_one(0)
+        gained(th1[0], ta_banks[0], 0)
+        gained(h1[3], a_banks[3], 3)
+        gate(3)
+        less_one(1)
         for t in range(PACK):
-            if t + 1 < PACK:
-                gained(th1[t + 1], ta_banks[t + 1], t + 1)
+            if t > 0:
+                gained(th1[t], ta_banks[t], t)
             nc.vector.tensor_tensor(part[:, t, :], th1[t][:].indirect(pick3[:]), slope[:, t, :], ALU.mult)
             if t > 0:
                 nc.vector.tensor_tensor(total[:, t - 1, :], th1[t - 1][:].indirect(pick2[:]), part[:, t - 1, :], ALU.add)
-        deal(nc.scalar.copy, wor_bf, wor_hi, P // 2, P, P // 2)
         for t in range(PACK):
             nc.scalar.activation(out=sig_rs[:, t, :], in_=sig[:, t, :], func=ACT.Copy, scale=rs_sb[:, t : t + 1])
-        nc.vector.quantize_mx(out=wor_q[:].bitcast(FP8X4), scales=wor_s[:],
-                              in_=wor_bf[:].rearrange("p t m j -> p (t m j)"))
+        deal(nc.scalar.copy, wor_bf, wor_hi, P // 2, P, P // 2)
         nc.vector.tensor_tensor(total[:, PACK - 1, :], th1[PACK - 1][:].indirect(pick2[:]), part[:, PACK - 1, :], ALU.add)
 
-        fo_bf = pool.tile([P, M, PACK], BF16, align_bytes=64, tag="wor_bf")
+        fo_bf = pool.tile([P, M, PACK], BF16, align_bytes=64, tag="fo_bf")
         fo_q = pool.tile([P, M], U32, align_bytes=64)
         fo_s = pool.tile([P, M], U8, align_bytes=64)
         nc.vector.tensor_tensor(fo_bf[:].rearrange("p (c i) t -> p c t i", i=4),
                                 total[:].rearrange("p t (c i) -> p c t i", i=4),
                                 sig_rs[:].rearrange("p t (c i) -> p c t i", i=4), ALU.mult)
-        nc.vector.quantize_mx(out=fo_q[:].bitcast(FP8X4), scales=fo_s[:], in_=fo_bf[:].rearrange("p m t -> p (m t)"))
 
-        yo = psum.tile([P, PACK, M], F32, name="a0", tag="a0")
-        for t in range(PACK):
-            cols = slice(t * P, (t + 1) * P)
-            nc.tensor.matmul_mx(out=yo[:, t, :], lhsT=wor_q[:, cols].bitcast(FP8X4), lhsT_scale=wor_s[:, cols],
-                                rhs=fo_q[:].bitcast(FP8X4), rhs_scale=fo_s[:], start=True, stop=True)
+        def quantise_wor(pair, tag):
+            codes = pool.tile([P, 2 * P], U32, name="wor_q%d" % pair, tag=tag, align_bytes=64)
+            scales = pool.tile([P, 2 * P], U8, name="wor_s%d" % pair, align_bytes=64)
+            nc.vector.quantize_mx(out=codes[:].bitcast(FP8X4), scales=scales[:],
+                                  in_=wor_bf[:, 2 * pair : 2 * pair + 2].rearrange("p t m j -> p (t m j)"))
+            return codes, scales
+
+        wor_mx = [quantise_wor(0, "wor_q0")]
+        nc.vector.quantize_mx(out=fo_q[:].bitcast(FP8X4), scales=fo_s[:], in_=fo_bf[:].rearrange("p m t -> p (m t)"))
+        wor_mx.append(quantise_wor(1, "fo_bf"))
+
         y = pool.tile([P, PACK, M], F32, align_bytes=64)
-        nc.vector.tensor_tensor(y[:], yo[:], res_sb[:], ALU.add)
+        for pair in range(2):
+            codes, scales = wor_mx[pair]
+            yo = psum.tile([P, 2, M], F32, name="a%d" % pair, tag="a%d" % pair)
+            for i in range(2):
+                cols = slice(i * P, (i + 1) * P)
+                nc.tensor.matmul_mx(out=yo[:, i, :], lhsT=codes[:, cols].bitcast(FP8X4), lhsT_scale=scales[:, cols],
+                                    rhs=fo_q[:].bitcast(FP8X4), rhs_scale=fo_s[:], start=True, stop=True)
+            rows = slice(2 * pair, 2 * pair + 2)
+            nc.vector.tensor_tensor(y[:, rows, :], yo[:], res_sb[:, rows, :], ALU.add)
         nc.sync.dma_start(out=out_0.rearrange("(p t) m -> p t m", t=PACK), in_=y[:])
         y_bf = pool.tile([P, M, PACK], BF16, align_bytes=64)
         y_q = pool.tile([P, M], U32, align_bytes=64)

@@ -17,9 +17,10 @@ ACT = mybir.ActivationFunctionType
 
 P = 128
 PACK = 4
-W1_SPLIT = 96
-DTAB_ROW = 4
+W1_SPLIT = 80
+WOR_SPLIT = 56
 HALF = J // 2
+ROW0 = P - 16
 
 
 def deal(engine_copy, dealt, raw, lo, hi, first=0):
@@ -39,57 +40,64 @@ def tile_attend_tpairgates_o_pl_kernel(tc, dtab_words, dtab_scales, tab_words, t
         slot_list = pool.tile([P, J // 16], U16)
         pick2 = pool.tile([P, M // 16], U16)
         pick3 = pool.tile([P, M // 16], U16)
-        tab_w = pool.tile([P, T], U32, align_bytes=64, tag="tab_w")
+        tab_w = pool.tile([P, T], U32, align_bytes=64)
         dtab_w = pool.tile([P, T], U32, align_bytes=64, tag="dtab_w")
-        tab_s = pool.tile([P, T], U8, align_bytes=64, tag="tab_s")
+        tab_s = pool.tile([P, T], U8, align_bytes=64)
         dtab_s = pool.tile([P, T], U8, align_bytes=64)
         w1_raw = pool.tile([P, PACK, R], F32, align_bytes=64)
-        wor_lo = pool.tile([P, PACK, F // 2], F32, align_bytes=64, tag="h1_1")
-        wor_hi = pool.tile([P, PACK, F // 2], F32, align_bytes=64)
-        wor_rows = wor.rearrange("(p j) c -> p j c", j=PACK)
+        wor_raw = pool.tile([P, PACK, F], F32, align_bytes=64)
         res_sb = pool.tile([P, PACK, M], F32, align_bytes=64)
         gain_sb = pool.tile([P, PACK], F32)
         rs_sb = pool.tile([P, PACK], F32)
 
         warm = pool.tile([P, 1], F32)
         warm_out = pool.tile([P, 1], F32)
-        nc.vector.memset(tab_s[:].bitcast(I32), 0)
-        nc.vector.memset(dtab_s[:].bitcast(I32), 0)
-        nc.vector.memset(warm[:], 0.0)
-
-        nc.sync.dma_start(out=w1_raw[:], in_=w1.rearrange("(p j) c -> p j c", j=PACK))
-        nc.sync.dma_start(slot_list[:], offs)
-        nc.sync.dma_start(pick3[:], offs3)
-        nc.scalar.activation(out=warm_out[:], in_=warm[:], func=ACT.Sigmoid)
-        for q in range(4):
-            nc.sync.dma_start(out=tab_s[32 * q : 32 * q + 4, :].bitcast(I32),
-                              in_=tab_scales[0, 4 * q : 4 * q + 4, :].bitcast(I32))
-        nc.sync.dma_start(out=tab_w[:].bitcast(I32), in_=tab_words[0].rearrange("p n t -> p (n t)").bitcast(I32))
-        nc.sync.dma_start(out=wor_lo[:], in_=wor_rows[:, :, 0 : F // 2])
-        for q in range(4):
-            nc.sync.dma_start(out=dtab_s[32 * q + DTAB_ROW : 32 * q + DTAB_ROW + 4, :].bitcast(I32),
-                              in_=dtab_scales[0, 4 * q : 4 * q + 4, :].bitcast(I32))
-        nc.sync.dma_start(out=gain_sb[:], in_=gain.rearrange("(p t) o -> p (t o)", t=PACK))
-        nc.sync.dma_start(out=dtab_w[:].bitcast(I32), in_=dtab_words[0].rearrange("p n t -> p (n t)").bitcast(I32))
-        nc.sync.dma_start(pick2[:], offs2)
-        nc.sync.dma_start(out=wor_hi[:], in_=wor_rows[:, :, F // 2 : F])
-        nc.sync.dma_start(out=res_sb[:], in_=res.rearrange("(p t) m -> p t m", t=PACK))
-        nc.sync.dma_start(out=rs_sb[:], in_=rs.rearrange("(p t) o -> p (t o)", t=PACK))
-
         tab_gw = pool.tile([P, J], U32, align_bytes=64)
         dtab_gw = pool.tile([P, J], U32, align_bytes=64, tag="h1_3")
         tab_gs = pool.tile([P, J], U8, align_bytes=64)
+        dtab_gs = pool.tile([P, J], U8, align_bytes=64)
+        tab_pl = pool.tile([P, J], U8, align_bytes=64)
+        dtab_pl = pool.tile([P, J], U8, align_bytes=64)
+
+        nc.vector.memset(tab_s[0:ROW0, :].bitcast(I32), 0)
+        nc.vector.memset(warm[:], 0.0)
+        nc.vector.memset(dtab_s[0:ROW0, :].bitcast(I32), 0)
+        nc.vector.memset(tab_pl[:].bitcast(I32), 0)
+        nc.vector.memset(dtab_pl[:].bitcast(I32), 0)
+
+        nc.sync.dma_start(slot_list[:], offs)
+        nc.sync.dma_start(out=w1_raw[:], in_=w1.rearrange("(p j) c -> p j c", j=PACK))
+        nc.scalar.dma_start(out=tab_s[ROW0:P, :].bitcast(I32), in_=tab_scales[0].bitcast(I32))
+        nc.scalar.dma_start(out=dtab_s[ROW0:P, :].bitcast(I32), in_=dtab_scales[0].bitcast(I32))
+        nc.scalar.dma_start(out=gain_sb[:], in_=gain.rearrange("(p t) o -> p (t o)", t=PACK))
+        nc.scalar.activation(out=warm_out[:], in_=warm[:], func=ACT.Sigmoid)
+        nc.sync.dma_start(out=tab_w[:].bitcast(I32), in_=tab_words[0].rearrange("p n t -> p (n t)").bitcast(I32))
+        nc.sync.dma_start(pick3[:], offs3)
+
+        def place_scales(rows, plane):
+            for q in range(4):
+                nc.sync.dma_start(out=plane[32 * q : 32 * q + 4, :].bitcast(I32),
+                                  in_=rows[ROW0 + 4 * q : ROW0 + 4 * q + 4, :].bitcast(I32))
 
         nc.vector.tensor_copy(tab_gs[:], tab_s[:].indirect(slot_list[:]))
+        nc.vector.tensor_copy(dtab_gs[:], dtab_s[:].indirect(slot_list[:]))
+        place_scales(tab_gs, tab_pl)
+        nc.sync.dma_start(out=dtab_w[:].bitcast(I32), in_=dtab_words[0].rearrange("p n t -> p (n t)").bitcast(I32))
+        place_scales(dtab_gs, dtab_pl)
+        nc.sync.dma_start(pick2[:], offs2)
+        nc.sync.dma_start(out=wor_raw[:], in_=wor.rearrange("(p j) c -> p j c", j=PACK))
+        nc.sync.dma_start(out=res_sb[:], in_=res.rearrange("(p t) m -> p t m", t=PACK))
+        nc.sync.dma_start(out=rs_sb[:], in_=rs.rearrange("(p t) o -> p (t o)", t=PACK))
+
         w1_bf = pool.tile([P, PACK, P, PACK], BF16, align_bytes=64)
-        w1_q = pool.tile([P, R], U32, align_bytes=64, tag="tab_s")
+        w1_q = pool.tile([P, R], U32, align_bytes=64)
         w1_s = pool.tile([P, R], U8, align_bytes=64)
         deal(nc.scalar.copy, w1_bf, w1_raw, 0, W1_SPLIT)
         deal(nc.vector.tensor_copy, w1_bf, w1_raw, W1_SPLIT, P)
         nc.vector.quantize_mx(out=w1_q[:].bitcast(FP8X4), scales=w1_s[:],
                               in_=w1_bf[:].rearrange("p t m j -> p (t m j)"))
 
-        def first_layer(table, words, scales, row, tag):
+        def first_layer(table, words, scales, tag):
             banks = [psum.tile([P, J], F32, name="%s%d" % (tag, t), tag="%s%d" % (tag, t)) for t in range(PACK)]
             for half in range(2):
                 slots = slice(half * HALF, (half + 1) * HALF)
@@ -98,12 +106,11 @@ def tile_attend_tpairgates_o_pl_kernel(tc, dtab_words, dtab_scales, tab_words, t
                 for t in range(PACK):
                     cols = slice(t * P, (t + 1) * P)
                     nc.tensor.matmul_mx(out=banks[t][:, slots], lhsT=w1_q[:, cols].bitcast(FP8X4), lhsT_scale=w1_s[:, cols],
-                                        rhs=words[:, slots].bitcast(FP8X4), rhs_scale=scales[row:P, slots],
+                                        rhs=words[:, slots].bitcast(FP8X4), rhs_scale=scales[:, slots],
                                         start=True, stop=True)
             return banks
 
         wor_bf = pool.tile([P, PACK, P, PACK], BF16, align_bytes=64)
-        deal(nc.scalar.copy, wor_bf, wor_lo, 0, P // 2)
         h1 = [pool.tile([P, J], F32, name="h1_%d" % t, tag="h1_%d" % t, align_bytes=64) for t in range(PACK - 1)]
         th1 = [pool.tile([P, J], F32, name="th1_%d" % t, align_bytes=64) for t in range(PACK)]
         sig = pool.tile([P, PACK, M], F32, align_bytes=64)
@@ -113,11 +120,9 @@ def tile_attend_tpairgates_o_pl_kernel(tc, dtab_words, dtab_scales, tab_words, t
         part = pool.tile([P, PACK, M], F32, align_bytes=64)
         total = pool.tile([P, PACK, M], F32, align_bytes=64)
 
-        a_banks = first_layer(tab_w, tab_gw, tab_gs, 0, "a")
-        dtab_gs = pool.tile([P, J], U8, align_bytes=64, tag="tab_w")
-        nc.vector.tensor_copy(dtab_gs[:], dtab_s[:].indirect(slot_list[:]))
+        a_banks = first_layer(tab_w, tab_gw, tab_pl, "a")
         nc.vector.tensor_scalar(h1[0][:], a_banks[0][:], gain_sb[:, 0:1], None, ALU.mult)
-        ta_banks = first_layer(dtab_w, dtab_gw, dtab_gs, DTAB_ROW, "ta")
+        ta_banks = first_layer(dtab_w, dtab_gw, dtab_pl, "ta")
         prod = pool.tile([P, PACK, M], F32, align_bytes=64, tag="dtab_w")
         h1.append(pool.tile([P, J], F32, name="h1_3", tag="h1_3", align_bytes=64))
 
@@ -142,6 +147,7 @@ def tile_attend_tpairgates_o_pl_kernel(tc, dtab_words, dtab_scales, tab_words, t
         gained(h1[3], a_banks[3], 3)
         gate(3)
         less_one(1)
+        deal(nc.vector.tensor_copy, wor_bf, wor_raw, 0, WOR_SPLIT)
         for t in range(PACK):
             if t > 0:
                 gained(th1[t], ta_banks[t], t)
@@ -150,7 +156,7 @@ def tile_attend_tpairgates_o_pl_kernel(tc, dtab_words, dtab_scales, tab_words, t
                 nc.vector.tensor_tensor(total[:, t - 1, :], th1[t - 1][:].indirect(pick2[:]), part[:, t - 1, :], ALU.add)
         for t in range(PACK):
             nc.scalar.activation(out=sig_rs[:, t, :], in_=sig[:, t, :], func=ACT.Copy, scale=rs_sb[:, t : t + 1])
-        deal(nc.scalar.copy, wor_bf, wor_hi, P // 2, P, P // 2)
+        deal(nc.scalar.copy, wor_bf, wor_raw, WOR_SPLIT, P)
         nc.vector.tensor_tensor(total[:, PACK - 1, :], th1[PACK - 1][:].indirect(pick2[:]), part[:, PACK - 1, :], ALU.add)
 
         fo_bf = pool.tile([P, M, PACK], BF16, align_bytes=64, tag="fo_bf")

from contextlib import ExitStack

import concourse.mybir as mybir

K, R, F, T, J, M = 512, 512, 512, 2048, 512, 128
FLOPS = 2 * (2 * K * R * J + R * F * M)

F32 = mybir.dt.float32
BF16 = mybir.dt.bfloat16
I32 = mybir.dt.int32
U32 = mybir.dt.uint32
U16 = mybir.dt.uint16
U8 = mybir.dt.uint8
FP8X4 = mybir.dt.float8_e4m3fn_x4
ALU = mybir.AluOpType
ACT = mybir.ActivationFunctionType

P = 128
PACK = 4
W1_SPLIT = 80
WOR_SPLIT = 56
HALF = J // 2
ROW0 = P - 16


def deal(engine_copy, dealt, raw, lo, hi, first=0):
    engine_copy(
        out=dealt[:].rearrange("p t m j -> p m j t")[:, lo:hi],
        in_=raw[:].rearrange("p j (m t) -> p m j t", t=PACK)[:, lo - first : hi - first],
    )


def tile_attend_tpairgates_o_pl_kernel(tc, dtab_words, dtab_scales, tab_words, tab_scales, w1, gain, rs, wor, res,
                                        offs, offs2, offs3, out_0, out_1, out_2):
    nc = tc.nc
    with ExitStack() as ctx:
        pool = ctx.enter_context(tc.tile_pool(name="keep", bufs=1))
        psum = ctx.enter_context(tc.psum_pool(name="psum", bufs=1))

        slot_list = pool.tile([P, J // 16], U16)
        pick2 = pool.tile([P, M // 16], U16)
        pick3 = pool.tile([P, M // 16], U16)
        tab_w = pool.tile([P, T], U32, align_bytes=64)
        dtab_w = pool.tile([P, T], U32, align_bytes=64, tag="dtab_w")
        tab_s = pool.tile([P, T], U8, align_bytes=64)
        dtab_s = pool.tile([P, T], U8, align_bytes=64)
        w1_raw = pool.tile([P, PACK, R], F32, align_bytes=64)
        wor_raw = pool.tile([P, PACK, F], F32, align_bytes=64)
        res_sb = pool.tile([P, PACK, M], F32, align_bytes=64)
        gain_sb = pool.tile([P, PACK], F32)
        rs_sb = pool.tile([P, PACK], F32)

        warm = pool.tile([P, 1], F32)
        warm_out = pool.tile([P, 1], F32)
        tab_gw = pool.tile([P, J], U32, align_bytes=64)
        dtab_gw = pool.tile([P, J], U32, align_bytes=64, tag="h1_3")
        tab_gs = pool.tile([P, J], U8, align_bytes=64)
        dtab_gs = pool.tile([P, J], U8, align_bytes=64)
        tab_pl = pool.tile([P, J], U8, align_bytes=64)
        dtab_pl = pool.tile([P, J], U8, align_bytes=64)

        nc.vector.memset(tab_s[0:ROW0, :].bitcast(I32), 0)
        nc.vector.memset(warm[:], 0.0)
        nc.vector.memset(dtab_s[0:ROW0, :].bitcast(I32), 0)
        nc.vector.memset(tab_pl[:].bitcast(I32), 0)
        nc.vector.memset(dtab_pl[:].bitcast(I32), 0)

        nc.sync.dma_start(slot_list[:], offs)
        nc.sync.dma_start(out=w1_raw[:], in_=w1.rearrange("(p j) c -> p j c", j=PACK))
        nc.scalar.dma_start(out=tab_s[ROW0:P, :].bitcast(I32), in_=tab_scales[0].bitcast(I32))
        nc.scalar.dma_start(out=dtab_s[ROW0:P, :].bitcast(I32), in_=dtab_scales[0].bitcast(I32))
        nc.scalar.dma_start(out=gain_sb[:], in_=gain.rearrange("(p t) o -> p (t o)", t=PACK))
        nc.scalar.activation(out=warm_out[:], in_=warm[:], func=ACT.Sigmoid)
        nc.sync.dma_start(out=tab_w[:].bitcast(I32), in_=tab_words[0].rearrange("p n t -> p (n t)").bitcast(I32))
        nc.sync.dma_start(pick3[:], offs3)

        def place_scales(rows, plane):
            for q in range(4):
                nc.sync.dma_start(out=plane[32 * q : 32 * q + 4, :].bitcast(I32),
                                  in_=rows[ROW0 + 4 * q : ROW0 + 4 * q + 4, :].bitcast(I32))

        nc.vector.tensor_copy(tab_gs[:], tab_s[:].indirect(slot_list[:]))
        nc.vector.tensor_copy(dtab_gs[:], dtab_s[:].indirect(slot_list[:]))
        place_scales(tab_gs, tab_pl)
        nc.sync.dma_start(out=dtab_w[:].bitcast(I32), in_=dtab_words[0].rearrange("p n t -> p (n t)").bitcast(I32))
        place_scales(dtab_gs, dtab_pl)
        nc.sync.dma_start(pick2[:], offs2)
        nc.sync.dma_start(out=wor_raw[:], in_=wor.rearrange("(p j) c -> p j c", j=PACK))
        nc.sync.dma_start(out=res_sb[:], in_=res.rearrange("(p t) m -> p t m", t=PACK))
        nc.sync.dma_start(out=rs_sb[:], in_=rs.rearrange("(p t) o -> p (t o)", t=PACK))

        w1_bf = pool.tile([P, PACK, P, PACK], BF16, align_bytes=64)
        w1_q = pool.tile([P, R], U32, align_bytes=64)
        w1_s = pool.tile([P, R], U8, align_bytes=64)
        deal(nc.scalar.copy, w1_bf, w1_raw, 0, W1_SPLIT)
        deal(nc.vector.tensor_copy, w1_bf, w1_raw, W1_SPLIT, P)
        nc.vector.quantize_mx(out=w1_q[:].bitcast(FP8X4), scales=w1_s[:],
                              in_=w1_bf[:].rearrange("p t m j -> p (t m j)"))

        def first_layer(table, words, scales, tag):
            banks = [psum.tile([P, J], F32, name="%s%d" % (tag, t), tag="%s%d" % (tag, t)) for t in range(PACK)]
            for half in range(2):
                slots = slice(half * HALF, (half + 1) * HALF)
                nc.vector.tensor_copy(words[:, slots],
                                      table[:].indirect(slot_list[:, half * HALF // 16 : (half + 1) * HALF // 16]))
                for t in range(PACK):
                    cols = slice(t * P, (t + 1) * P)
                    nc.tensor.matmul_mx(out=banks[t][:, slots], lhsT=w1_q[:, cols].bitcast(FP8X4), lhsT_scale=w1_s[:, cols],
                                        rhs=words[:, slots].bitcast(FP8X4), rhs_scale=scales[:, slots],
                                        start=True, stop=True)
            return banks

        wor_bf = pool.tile([P, PACK, P, PACK], BF16, align_bytes=64)
        h1 = [pool.tile([P, J], F32, name="h1_%d" % t, tag="h1_%d" % t, align_bytes=64) for t in range(PACK - 1)]
        th1 = [pool.tile([P, J], F32, name="th1_%d" % t, align_bytes=64) for t in range(PACK)]
        sig = pool.tile([P, PACK, M], F32, align_bytes=64)
        rest = pool.tile([P, PACK, M], F32, align_bytes=64)
        sig_rs = pool.tile([P, PACK, M], F32, align_bytes=64)
        slope = pool.tile([P, PACK, M], F32, align_bytes=64)
        part = pool.tile([P, PACK, M], F32, align_bytes=64)
        total = pool.tile([P, PACK, M], F32, align_bytes=64)

        a_banks = first_layer(tab_w, tab_gw, tab_pl, "a")
        nc.vector.tensor_scalar(h1[0][:], a_banks[0][:], gain_sb[:, 0:1], None, ALU.mult)
        ta_banks = first_layer(dtab_w, dtab_gw, dtab_pl, "ta")
        prod = pool.tile([P, PACK, M], F32, align_bytes=64, tag="dtab_w")
        h1.append(pool.tile([P, J], F32, name="h1_3", tag="h1_3", align_bytes=64))

        def gained(dst, bank, t):
            nc.scalar.activation(out=dst[:], in_=bank[:], func=ACT.Copy, scale=gain_sb[:, t : t + 1])

        def gate(t):
            nc.scalar.activation(out=sig[:, t, :], in_=h1[t][:].indirect(pick3[:]), func=ACT.Sigmoid)
            nc.scalar.activation(out=rest[:, t, :], in_=sig[:, t, :], func=ACT.Copy, scale=-1.0, bias=1.0)
            nc.vector.tensor_tensor(prod[:, t, :], h1[t][:].indirect(pick2[:]), rest[:, t, :], ALU.mult)

        def less_one(pair):
            rows = slice(2 * pair, 2 * pair + 2)
            nc.vector.tensor_scalar(slope[:, rows, :], prod[:, rows, :], -1.0, None, ALU.add)

        gained(h1[1], a_banks[1], 1)
        gained(h1[2], a_banks[2], 2)
        for t in range(PACK - 1):
            gate(t)
        less_one(0)
        gained(th1[0], ta_banks[0], 0)
        gained(h1[3], a_banks[3], 3)
        gate(3)
        less_one(1)
        deal(nc.vector.tensor_copy, wor_bf, wor_raw, 0, WOR_SPLIT)
        for t in range(PACK):
            if t > 0:
                gained(th1[t], ta_banks[t], t)
            nc.vector.tensor_tensor(part[:, t, :], th1[t][:].indirect(pick3[:]), slope[:, t, :], ALU.mult)
            if t > 0:
                nc.vector.tensor_tensor(total[:, t - 1, :], th1[t - 1][:].indirect(pick2[:]), part[:, t - 1, :], ALU.add)
        for t in range(PACK):
            nc.scalar.activation(out=sig_rs[:, t, :], in_=sig[:, t, :], func=ACT.Copy, scale=rs_sb[:, t : t + 1])
        deal(nc.scalar.copy, wor_bf, wor_raw, WOR_SPLIT, P)
        nc.vector.tensor_tensor(total[:, PACK - 1, :], th1[PACK - 1][:].indirect(pick2[:]), part[:, PACK - 1, :], ALU.add)

        fo_bf = pool.tile([P, M, PACK], BF16, align_bytes=64, tag="fo_bf")
        fo_q = pool.tile([P, M], U32, align_bytes=64)
        fo_s = pool.tile([P, M], U8, align_bytes=64)
        nc.vector.tensor_tensor(fo_bf[:].rearrange("p (c i) t -> p c t i", i=4),
                                total[:].rearrange("p t (c i) -> p c t i", i=4),
                                sig_rs[:].rearrange("p t (c i) -> p c t i", i=4), ALU.mult)

        def quantise_wor(pair, tag):
            codes = pool.tile([P, 2 * P], U32, name="wor_q%d" % pair, tag=tag, align_bytes=64)
            scales = pool.tile([P, 2 * P], U8, name="wor_s%d" % pair, align_bytes=64)
            nc.vector.quantize_mx(out=codes[:].bitcast(FP8X4), scales=scales[:],
                                  in_=wor_bf[:, 2 * pair : 2 * pair + 2].rearrange("p t m j -> p (t m j)"))
            return codes, scales

        wor_mx = [quantise_wor(0, "wor_q0")]
        nc.vector.quantize_mx(out=fo_q[:].bitcast(FP8X4), scales=fo_s[:], in_=fo_bf[:].rearrange("p m t -> p (m t)"))
        wor_mx.append(quantise_wor(1, "fo_bf"))

        y = pool.tile([P, PACK, M], F32, align_bytes=64)
        for pair in range(2):
            codes, scales = wor_mx[pair]
            yo = psum.tile([P, 2, M], F32, name="a%d" % pair, tag="a%d" % pair)
            for i in range(2):
                cols = slice(i * P, (i + 1) * P)
                nc.tensor.matmul_mx(out=yo[:, i, :], lhsT=codes[:, cols].bitcast(FP8X4), lhsT_scale=scales[:, cols],
                                    rhs=fo_q[:].bitcast(FP8X4), rhs_scale=fo_s[:], start=True, stop=True)
            rows = slice(2 * pair, 2 * pair + 2)
            nc.vector.tensor_tensor(y[:, rows, :], yo[:], res_sb[:, rows, :], ALU.add)
        nc.sync.dma_start(out=out_0.rearrange("(p t) m -> p t m", t=PACK), in_=y[:])
        y_bf = pool.tile([P, M, PACK], BF16, align_bytes=64)
        y_q = pool.tile([P, M], U32, align_bytes=64)
        y_s = pool.tile([P, M], U8, align_bytes=64)
        nc.vector.tensor_copy(y_bf[:].rearrange("p (c i) t -> p c t i", i=4), y[:].rearrange("p t (c i) -> p c t i", i=4))
        nc.vector.quantize_mx(out=y_q[:].bitcast(FP8X4), scales=y_s[:], in_=y_bf[:].rearrange("p m t -> p (m t)"))
        nc.sync.dma_start(out=out_1[0].rearrange("p c t -> p (c t)").bitcast(I32), in_=y_q[:].bitcast(I32))
        for q in range(4):
            queue = nc.scalar if q % 2 == 0 else nc.sync
            queue.dma_start(out=out_2[0, 4 * q : 4 * q + 4, :].bitcast(I32), in_=y_s[32 * q : 32 * q + 4, :].bitcast(I32))
